import numpy as np
import ml_dtypes


def mxq(x, axis, fmt="e4m3"):
    dtype, down = {"e4m3": (ml_dtypes.float8_e4m3fn, 7), "e5m2": (ml_dtypes.float8_e5m2, 14)}[fmt]
    v = np.moveaxis(np.asarray(x, np.float32).astype(ml_dtypes.bfloat16).astype(np.float64), axis, -1)
    blocks = v.reshape(v.shape[:-1] + (-1, 32))
    amax = np.abs(blocks).max(-1, keepdims=True)
    byte = np.maximum(np.where(amax > 0, np.frexp(amax)[1] - 1 + 127, 0) - down, 1)
    scale = np.exp2(byte - 127.0)
    codes = (blocks / scale).astype(np.float32).astype(dtype).astype(np.float64)
    return np.moveaxis((codes * scale).reshape(v.shape), -1, axis)


WIDE = False


def mx_kscale(k):
    if not WIDE:
        return np.ones(k)
    levels = np.array([10, -10, 5, -5, 0])
    if k % 512:
        return np.exp2(np.random.permutation(np.resize(levels, k // 32))).repeat(32)
    a = np.empty((k // 512, 16))
    for p in range(k // 512):
        a[p, :8] = np.random.permutation(np.resize(levels, 8))
        for g in range(8):
            far = levels[np.abs(levels - a[p, g]) >= 10]
            a[p, g + 8] = far[np.random.randint(len(far))]
    return np.exp2(a.ravel()).repeat(32)


BF16 = ml_dtypes.bfloat16


def bf(x):
    return np.asarray(x, np.float32).astype(BF16)


def f64(x):
    return np.asarray(x).astype(np.float64)


E2M1 = np.array([0.0, 0.5, 1.0, 1.5, 2.0, 3.0, 4.0, 6.0, -0.0, -0.5, -1.0, -1.5, -2.0, -3.0, -4.0, -6.0])


def pack_weight(w, fmt):
    k, n = w.shape
    w = f64(bf(w)).reshape(k // 32, 32, n)
    amax = np.abs(w).max(1)
    if fmt == "e4m3":
        byte = np.frexp(amax)[1] - 1 + 127 - 7
    else:
        mant, ex = np.frexp(amax / 6.0)
        byte = np.where(mant > 0.5, ex, ex - 1) + 127
    byte = np.clip(np.where(amax > 0, byte, 1), 1, 254)
    scaled = (w * np.exp2(127.0 - byte)[:, None, :]).reshape(k, n).astype(np.float32)
    by_word = np.ascontiguousarray(scaled.reshape(k // 512, 128, 4, n).transpose(0, 1, 3, 2))
    if fmt == "e4m3":
        words = by_word.astype(ml_dtypes.float8_e4m3fn).view(np.uint8)
    else:
        c = by_word.astype(ml_dtypes.float4_e2m1fn).view(np.uint8) & 0xF
        words = c[..., 0::2] | (c[..., 1::2] << 4)
    return np.ascontiguousarray(words), np.ascontiguousarray(byte.astype(np.uint8).reshape(k // 512, 16, n))


def unpack_weight(words, scales, fmt):
    g, p, n, _ = words.shape
    if fmt == "e4m3":
        vals = np.ascontiguousarray(words).view(ml_dtypes.float8_e4m3fn).astype(np.float64)
    else:
        nib = np.empty((g, p, n, 4), np.uint8)
        nib[..., 0::2] = words & 0xF
        nib[..., 1::2] = words >> 4
        vals = E2M1[nib]
    vals = vals * np.repeat(np.exp2(scales.astype(np.float64) - 127.0), 8, axis=1)[..., None]
    return vals.transpose(0, 1, 3, 2).reshape(g * 512, n)
def pack4(w):
    words, scales = pack_weight(w, "e2m1")
    return words.reshape(words.shape[0], 128, -1), scales


def unpack4(words, scales):
    return unpack_weight(words.reshape(words.shape[0], 128, -1, 2), scales, "e2m1")


N, R = 2048, 512


def setup_inputs():
    s = mx_kscale(N)
    m = (1 + 0.15 * np.random.standard_normal(N)) * s
    a = np.random.standard_normal((N, N))
    b = (a + a.T) / np.sqrt(2 * N)
    w_words, w_scales = pack4(b / s[:, None] / s)
    e = np.sign(np.random.standard_normal((N, R)))
    return {"w_words": w_words,
            "w_scales": w_scales,
            "d": bf(m * m),
            "z": bf(e * m[:, None])}


def reference(w_words, w_scales, d, z):
    w = unpack4(w_words, w_scales)
    zf = f64(z)
    y = w.T @ mxq(zf, 0, "e4m3")
    x = f64(d)[:, None] * y
    v = w.T @ mxq(x, 0, "e4m3")
    c = zf * v
    return c, c.mean(1)

@@ -1,0 +1,236 @@
+from contextlib import ExitStack
+
+import concourse.mybir as mybir
+from concourse.masks import make_identity
+
+N, R = 2048, 512
+FLOPS = 2 * 2 * N * N * R
+
+F32 = mybir.dt.float32
+BF16 = mybir.dt.bfloat16
+I32 = mybir.dt.int32
+U32 = mybir.dt.uint32
+U8 = mybir.dt.uint8
+FP8X4 = mybir.dt.float8_e4m3fn_x4
+FP4X4 = mybir.dt.float4_e2m1fn_x4
+MULT = mybir.AluOpType.mult
+
+P = 128
+PACK = 4
+CHUNK = P * PACK
+PASSES = N // CHUNK
+R_TILES = R // P
+HALF = R // 2
+N_TILES = N // P
+BANKS = 8
+
+
+def tile_hutchinson_squared_diagonal_s13_kernel(tc, w_words, w_scales, d, z, out_0, out_1):
+    nc = tc.nc
+    with ExitStack() as ctx:
+        keep = ctx.enter_context(tc.tile_pool(name="keep", bufs=1))
+        stage = ctx.enter_context(tc.tile_pool(name="stage", bufs=6))
+        psum = ctx.enter_context(tc.psum_pool(name="psum", bufs=1))
+        ctx.enter_context(tc.manual_schedule())
+
+        def sb(name, shape, dtype):
+            return keep.tile(shape, dtype, name=name, align_bytes=64)
+
+        free_banks = [BANKS - 2, BANKS - 1] + list(range(BANKS - 2))
+
+        def take_bank(shape, dtype):
+            b = free_banks[0]
+            free_banks.remove(b)
+            return b, psum.tile(shape, dtype, name="bank%d" % b, tag="bank%d" % b)
+
+        d_rows = sb("d_rows", [P, N // P], BF16)
+        ws = [sb("ws%d" % h, [P, PASSES, N // 2], U8) for h in range(2)]
+        sums = sb("sums", [P, 32], F32)
+        ident = sb("ident", [P, P], F32)
+        z0_raw = [sb("z0_raw%d" % h, [P, PACK, HALF], BF16) for h in range(2)]
+        z_raw = [None] + [sb("z_raw%d" % g, [P, PACK, R], BF16) for g in range(1, PASSES)]
+        w_lo = [sb("w_lo%d" % g, [P, N], U8) for g in range(PASSES)]
+        w_hi = [sb("w_hi%d" % c, [P, PASSES, 2 * CHUNK], U8) for c in range(2)]
+        z_rows = [sb("z_rows%d" % c, [P, PACK, R], BF16) for c in range(PASSES)]
+
+        nc.vector.memset(ws[0][:].bitcast(I32), 0)
+        nc.vector.memset(ws[1][:].bitcast(I32), 0)
+        nc.vector.memset(sums[:], 0.0)
+        make_identity(nc, ident[:])
+
+        def z_pass(g):
+            return z[g * CHUNK:(g + 1) * CHUNK, :].rearrange("(p t) r -> p t r", t=PACK)
+
+        def load_scales(queue, h):
+            rows = w_scales.rearrange("g (q s) n -> s q g n", s=4)
+            for s in range(4):
+                queue.dma_start(out=ws[h][s:P:32].bitcast(I32),
+                                in_=rows[s][:, :, h * (N // 2):(h + 1) * (N // 2)].bitcast(I32))
+
+        for h in range(2):
+            nc.sync.dma_start(out=z0_raw[h][:], in_=z_pass(0)[:, :, h * HALF:(h + 1) * HALF])
+        nc.scalar.dma_start(out=d_rows[:], in_=d.rearrange("(p j) -> p j", p=P))
+        nc.sync.dma_start(out=w_lo[0][:].bitcast(I32), in_=w_words[0][:, 0:N].bitcast(I32))
+        load_scales(nc.scalar, 0)
+        for g in range(1, PASSES):
+            nc.sync.dma_start(out=z_raw[g][:], in_=z_pass(g))
+            nc.sync.dma_start(out=w_lo[g][:].bitcast(I32), in_=w_words[g][:, 0:N].bitcast(I32))
+        load_scales(nc.sync, 1)
+        for c in range(2):
+            cols = slice(N + c * 2 * CHUNK, N + (c + 1) * 2 * CHUNK)
+            nc.sync.dma_start(out=w_hi[c][:].bitcast(I32),
+                              in_=w_words.rearrange("g p b -> p g b")[:, :, cols].bitcast(I32))
+        for c in range(PASSES):
+            nc.sync.dma_start(out=z_rows[c][:],
+                              in_=z[c * CHUNK:(c + 1) * CHUNK, :].rearrange("(j p) r -> p j r", p=P))
+
+        def w_operand(g, n0, width):
+            h, n1 = divmod(n0, N // 2)
+            scale = ws[h][:, g, n1:n1 + width]
+            if h == 0:
+                return w_lo[g][:, 2 * n1:2 * (n1 + width)].bitcast(FP4X4), scale
+            c, n2 = divmod(n1, CHUNK)
+            return w_hi[c][:, g, 2 * n2:2 * (n2 + width)].bitcast(FP4X4), scale
+
+        d_all = sb("d_all", [P, PASSES, 2, 2 * P], BF16)
+        d_words = d_rows[:].bitcast(F32)
+        for u in range(2):
+            b, bank = take_bank([P, 4, P], F32)
+            for a in range(4):
+                w = 2 * a + u
+                nc.tensor.transpose(bank[:, a, :], d_words[:, w:w + 1].to_broadcast([P, P]), ident[:])
+            nc.scalar.copy(out=d_all[:, :, u, :].bitcast(F32).rearrange("m c (s a) -> m c s a", a=4),
+                           in_=bank[:].rearrange("m a (c s) -> m c s a", c=PASSES))
+            free_banks.append(b)
+
+        z_grouped = [[sb("z_grouped%d_%d" % (g, h), [P, HALF, PACK], BF16) for h in range(2)] for g in range(PASSES)]
+        z_codes = [[sb("z_codes%d_%d" % (g, h), [P, HALF], U32) for h in range(2)] for g in range(PASSES)]
+        z_scales = [[sb("z_scales%d_%d" % (g, h), [P, HALF], U8) for h in range(2)] for g in range(PASSES)]
+
+        def interleave(copy, dst, src):
+            copy(out=dst.rearrange("p (c i) t -> p c t i", i=4), in_=src.rearrange("p t (c i) -> p c t i", i=4))
+
+        def quantize(codes, scales, grouped):
+            nc.vector.quantize_mx(out=codes.bitcast(FP8X4), scales=scales, in_=grouped.rearrange("p r t -> p (r t)"))
+
+        for h in range(2):
+            for q in range(2):
+                cols = slice(q * P, (q + 1) * P)
+                interleave(nc.vector.tensor_copy, z_grouped[0][h][:, cols, :], z0_raw[h][:, :, cols])
+            for q in range(2):
+                cols = slice(q * P, (q + 1) * P)
+                quantize(z_codes[0][h][:, cols], z_scales[0][h][:, cols], z_grouped[0][h][:, cols, :])
+        for g in range(1, PASSES):
+            interleave(nc.vector.tensor_copy, z_grouped[g][0][:], z_raw[g][:, :, 0:HALF])
+            interleave(nc.scalar.copy, z_grouped[g][1][:], z_raw[g][:, :, HALF:R])
+            for h in range(2):
+                quantize(z_codes[g][h][:], z_scales[g][h][:], z_grouped[g][h][:])
+
+        x_t = [[sb("x_t%d_%d" % (c, i), [P, CHUNK], BF16) for i in range(R_TILES)] for c in range(PASSES)]
+        x_grouped = [[sb("x_grouped%d_%d" % (c, h), [P, HALF, PACK], BF16) for h in range(2)] for c in range(PASSES)]
+        x_codes = [sb("x_codes%d" % c, [P, R], U32) for c in range(PASSES)]
+        x_scales = [sb("x_scales%d" % c, [P, R], U8) for c in range(PASSES)]
+
+        def y_pass(bank, c, i, g):
+            h, q = divmod(i, 2)
+            cols = slice(q * P, (q + 1) * P)
+            w_codes, w_scale = w_operand(g, c * CHUNK, CHUNK)
+            nc.tensor.matmul_mx(out=bank[:], lhsT=z_codes[g][h][:, cols].bitcast(FP8X4), lhsT_scale=z_scales[g][h][:, cols],
+                                rhs=w_codes, rhs_scale=w_scale, start=(g == 0), stop=(g == PASSES - 1))
+
+        def y_out(b, bank, c, i):
+            nc.vector.tensor_tensor(
+                out=x_t[c][i][:].rearrange("r (u p e) -> r u p e", u=2, e=2),
+                in0=bank[:].rearrange("r (p u e) -> r u p e", u=2, e=2),
+                in1=d_all[:, c].rearrange("r u (p e) -> r u p e", e=2),
+                op=MULT)
+            free_banks.append(b)
+
+        def y_group(c, i):
+            b, bank = take_bank([P, CHUNK], F32)
+            for g in range(PASSES):
+                y_pass(bank, c, i, g)
+            y_out(b, bank, c, i)
+
+        def turn(c, copies):
+            for h in range(2):
+                b, bank = take_bank([P, 2, 2, P], F32)
+                for q in range(2):
+                    words = x_t[c][2 * h + q][:].bitcast(F32)
+                    for u in range(2):
+                        nc.tensor.transpose(bank[:, q, u, :], words[:, u * P:(u + 1) * P], ident[:])
+                copies[h](out=x_grouped[c][h][:].bitcast(F32).rearrange("p (q r) u -> p q r u", q=2),
+                          in_=bank[:].rearrange("p q u r -> p q r u"))
+                free_banks.append(b)
+
+        def quantize_x(c):
+            for h in range(2):
+                cols = slice(h * HALF, (h + 1) * HALF)
+                quantize(x_codes[c][:, cols], x_scales[c][:, cols], x_grouped[c][h][:])
+
+        sweep = {}
+        for i in range(R_TILES):
+            for c in range(2):
+                sweep[c, i] = take_bank([P, CHUNK], F32)
+        for g in range(PASSES - 1):
+            for i in range(R_TILES):
+                for c in range(2):
+                    y_pass(sweep[c, i][1], c, i, g)
+        for c in range(2):
+            for i in range(R_TILES):
+                y_pass(sweep[c, i][1], c, i, PASSES - 1)
+                y_out(*sweep[c, i], c, i)
+
+        on_scalar = [nc.scalar.copy, nc.scalar.copy]
+        for i in range(R_TILES - 1):
+            y_group(2, i)
+        turn(0, on_scalar)
+        turn(1, on_scalar)
+        quantize_x(0)
+        y_group(2, R_TILES - 1)
+        quantize_x(1)
+        y_group(3, 0)
+        y_group(3, 1)
+        turn(2, on_scalar)
+        quantize_x(2)
+        y_group(3, 2)
+        y_group(3, 3)
+
+        def v_pass(bank, j, g):
+            w_codes, w_scale = w_operand(g, j * P, P)
+            nc.tensor.matmul_mx(out=bank[:], lhsT=w_codes, lhsT_scale=w_scale,
+                                rhs=x_codes[g][:].bitcast(FP8X4), rhs_scale=x_scales[g][:],
+                                start=(g == 0), stop=(g == PASSES - 1))
+
+        def v_out(b, bank, j):
+            c_tile = stage.tile([P, R], F32, name="c_tile")
+            nc.vector.scalar_tensor_tensor(out=c_tile[:], in0=bank[:], scalar=1.0, in1=z_rows[j // PACK][:, j % PACK, :],
+                                           op0=MULT, op1=MULT, accum_out=sums[:, j:j + 1])
+            nc.sync.dma_start(out=out_0[j * P:(j + 1) * P, :], in_=c_tile[:])
+            free_banks.append(b)
+
+        early = []
+        for j in range(4):
+            early.append(take_bank([P, R], F32))
+            for g in range(PASSES - 1):
+                v_pass(early[j][1], j, g)
+            if j == 0:
+                turn(3, [nc.scalar.copy, nc.vector.tensor_copy])
+                quantize_x(3)
+        for j in range(4):
+            v_pass(early[j][1], j, PASSES - 1)
+            v_out(*early[j], j)
+        for j in range(4, N_TILES):
+            b, bank = take_bank([P, R], F32)
+            for g in range(PASSES):
+                v_pass(bank, j, g)
+            v_out(b, bank, j)
+
+        means = sb("means", [P, 32], F32)
+        means_t = sb("means_t", [P, 32], F32)
+        nc.vector.tensor_scalar(out=means[:], in0=sums[:], scalar1=1.0 / R, scalar2=None, op0=MULT)
+        nc.vector.transpose(means_t[:], means[:])
+        d_out = out_1.rearrange("(j q i) -> q j i", q=4, i=32)
+        for q in range(4):
+            queue = nc.scalar if q % 2 == 0 else nc.sync
+            queue.dma_start(out=d_out[q], in_=means_t[32 * q:32 * q + N_TILES, :])

@@ -23,6 +23,7 @@ R_TILES = R // P
 HALF = R // 2
 N_TILES = N // P
 BANKS = 8
+WARMUPS = 6
 
 
 def tile_hutchinson_squared_diagonal_s13_kernel(tc, w_words, w_scales, d, z, out_0, out_1):
@@ -36,7 +37,7 @@ def tile_hutchinson_squared_diagonal_s13_kernel(tc, w_words, w_scales, d, z, out
         def sb(name, shape, dtype):
             return keep.tile(shape, dtype, name=name, align_bytes=64)
 
-        free_banks = [BANKS - 2, BANKS - 1] + list(range(BANKS - 2))
+        free_banks = [BANKS - 3, BANKS - 2, BANKS - 1] + list(range(BANKS - 3))
 
         def take_bank(shape, dtype):
             b = free_banks[0]
@@ -44,7 +45,9 @@ def tile_hutchinson_squared_diagonal_s13_kernel(tc, w_words, w_scales, d, z, out
             return b, psum.tile(shape, dtype, name="bank%d" % b, tag="bank%d" % b)
 
         d_rows = sb("d_rows", [P, N // P], BF16)
-        ws = [sb("ws%d" % h, [P, PASSES, N // 2], U8) for h in range(2)]
+        ws_lo = [sb("ws_lo%d" % h, [P, 2, N // 2], U8) for h in range(2)]
+        ws_hi = sb("ws_hi", [P, PASSES, N // 2], U8)
+        warm = sb("warm", [P, CHUNK], BF16)
         sums = sb("sums", [P, 32], F32)
         ident = sb("ident", [P, P], F32)
         z0_raw = [sb("z0_raw%d" % h, [P, PACK, HALF], BF16) for h in range(2)]
@@ -53,29 +56,31 @@ def tile_hutchinson_squared_diagonal_s13_kernel(tc, w_words, w_scales, d, z, out
         w_hi = [sb("w_hi%d" % c, [P, PASSES, 2 * CHUNK], U8) for c in range(2)]
         z_rows = [sb("z_rows%d" % c, [P, PACK, R], BF16) for c in range(PASSES)]
 
-        nc.vector.memset(ws[0][:].bitcast(I32), 0)
-        nc.vector.memset(ws[1][:].bitcast(I32), 0)
+        nc.gpsimd.memset(warm[:].bitcast(I32), 0)
+        nc.vector.memset(ws_lo[0][:].bitcast(I32), 0)
+        nc.vector.memset(ws_lo[1][:].bitcast(I32), 0)
+        nc.vector.memset(ws_hi[:].bitcast(I32), 0)
         nc.vector.memset(sums[:], 0.0)
         make_identity(nc, ident[:])
 
         def z_pass(g):
             return z[g * CHUNK:(g + 1) * CHUNK, :].rearrange("(p t) r -> p t r", t=PACK)
 
-        def load_scales(queue, h):
+        def load_scales(plane, passes, cols):
             rows = w_scales.rearrange("g (q s) n -> s q g n", s=4)
             for s in range(4):
-                queue.dma_start(out=ws[h][s:P:32].bitcast(I32),
-                                in_=rows[s][:, :, h * (N // 2):(h + 1) * (N // 2)].bitcast(I32))
+                nc.sync.dma_start(out=plane[s:P:32].bitcast(I32), in_=rows[s][:, passes, cols].bitcast(I32))
 
+        nc.scalar.dma_start(out=d_rows[:], in_=d.rearrange("(p j) -> p j", p=P))
         for h in range(2):
             nc.sync.dma_start(out=z0_raw[h][:], in_=z_pass(0)[:, :, h * HALF:(h + 1) * HALF])
-        nc.scalar.dma_start(out=d_rows[:], in_=d.rearrange("(p j) -> p j", p=P))
-        nc.sync.dma_start(out=w_lo[0][:].bitcast(I32), in_=w_words[0][:, 0:N].bitcast(I32))
-        load_scales(nc.scalar, 0)
-        for g in range(1, PASSES):
-            nc.sync.dma_start(out=z_raw[g][:], in_=z_pass(g))
+        for g in range(PASSES):
+            if g > 0:
+                nc.sync.dma_start(out=z_raw[g][:], in_=z_pass(g))
+            if g % 2 == 0:
+                load_scales(ws_lo[g // 2], slice(g, g + 2), slice(0, N // 2))
             nc.sync.dma_start(out=w_lo[g][:].bitcast(I32), in_=w_words[g][:, 0:N].bitcast(I32))
-        load_scales(nc.sync, 1)
+        load_scales(ws_hi, slice(0, PASSES), slice(N // 2, N))
         for c in range(2):
             cols = slice(N + c * 2 * CHUNK, N + (c + 1) * 2 * CHUNK)
             nc.sync.dma_start(out=w_hi[c][:].bitcast(I32),
@@ -86,11 +91,15 @@ def tile_hutchinson_squared_diagonal_s13_kernel(tc, w_words, w_scales, d, z, out
 
         def w_operand(g, n0, width):
             h, n1 = divmod(n0, N // 2)
-            scale = ws[h][:, g, n1:n1 + width]
             if h == 0:
-                return w_lo[g][:, 2 * n1:2 * (n1 + width)].bitcast(FP4X4), scale
+                return w_lo[g][:, 2 * n1:2 * (n1 + width)].bitcast(FP4X4), ws_lo[g // 2][:, g % 2, n1:n1 + width]
             c, n2 = divmod(n1, CHUNK)
-            return w_hi[c][:, g, 2 * n2:2 * (n2 + width)].bitcast(FP4X4), scale
+            return w_hi[c][:, g, 2 * n2:2 * (n2 + width)].bitcast(FP4X4), ws_hi[:, g, n1:n1 + width]
+
+        b, bank = take_bank([P, CHUNK], F32)
+        for w in range(WARMUPS):
+            nc.tensor.matmul(bank[:], lhsT=warm[:, 0:P], rhs=warm[:], start=True, stop=True)
+        free_banks.append(b)
 
         d_all = sb("d_all", [P, PASSES, 2, 2 * P], BF16)
         d_words = d_rows[:].bitcast(F32)

@@ -23,7 +23,10 @@ R_TILES = R // P
 HALF = R // 2
 N_TILES = N // P
 BANKS = 8
-WARMUPS = 6
+WARMUPS = 4
+TURNED = PASSES - 1
+U16 = mybir.dt.uint16
+COPY = mybir.ActivationFunctionType.Copy
 
 
 def tile_hutchinson_squared_diagonal_s13_kernel(tc, w_words, w_scales, d, z, out_0, out_1):
@@ -44,14 +47,15 @@ def tile_hutchinson_squared_diagonal_s13_kernel(tc, w_words, w_scales, d, z, out
             free_banks.remove(b)
             return b, psum.tile(shape, dtype, name="bank%d" % b, tag="bank%d" % b)
 
-        d_rows = sb("d_rows", [P, N // P], BF16)
+        d_rows = sb("d_rows", [P, PACK * TURNED], BF16)
+        d_last = sb("d_last", [P, PACK], BF16)
+        d_last32 = sb("d_last32", [P, PACK], F32)
         ws_lo = [sb("ws_lo%d" % h, [P, 2, N // 2], U8) for h in range(2)]
         ws_hi = sb("ws_hi", [P, PASSES, N // 2], U8)
         warm = sb("warm", [P, CHUNK], BF16)
         sums = sb("sums", [P, 32], F32)
         ident = sb("ident", [P, P], F32)
-        z0_raw = [sb("z0_raw%d" % h, [P, PACK, HALF], BF16) for h in range(2)]
-        z_raw = [None] + [sb("z_raw%d" % g, [P, PACK, R], BF16) for g in range(1, PASSES)]
+        z_raw = [sb("z_raw%d" % g, [P, PACK, R], BF16) for g in range(PASSES)]
         w_lo = [sb("w_lo%d" % g, [P, N], U8) for g in range(PASSES)]
         w_hi = [sb("w_hi%d" % c, [P, PASSES, 2 * CHUNK], U8) for c in range(2)]
         z_rows = [sb("z_rows%d" % c, [P, PACK, R], BF16) for c in range(PASSES)]
@@ -71,12 +75,11 @@ def tile_hutchinson_squared_diagonal_s13_kernel(tc, w_words, w_scales, d, z, out
             for s in range(4):
                 nc.sync.dma_start(out=plane[s:P:32].bitcast(I32), in_=rows[s][:, passes, cols].bitcast(I32))
 
-        nc.scalar.dma_start(out=d_rows[:], in_=d.rearrange("(p j) -> p j", p=P))
-        for h in range(2):
-            nc.sync.dma_start(out=z0_raw[h][:], in_=z_pass(0)[:, :, h * HALF:(h + 1) * HALF])
+        nc.scalar.dma_start(out=d_rows[:], in_=d[0:TURNED * CHUNK].rearrange("(p j) -> p j", p=P))
+        nc.scalar.dma_start(out=d_last[:], in_=d[TURNED * CHUNK:N].rearrange("(p t) -> p t", p=P))
+        nc.scalar.activation(out=d_last32[:], in_=d_last[:], func=COPY)
         for g in range(PASSES):
-            if g > 0:
-                nc.sync.dma_start(out=z_raw[g][:], in_=z_pass(g))
+            nc.sync.dma_start(out=z_raw[g][:], in_=z_pass(g))
             if g % 2 == 0:
                 load_scales(ws_lo[g // 2], slice(g, g + 2), slice(0, N // 2))
             nc.sync.dma_start(out=w_lo[g][:].bitcast(I32), in_=w_words[g][:, 0:N].bitcast(I32))
@@ -101,20 +104,9 @@ def tile_hutchinson_squared_diagonal_s13_kernel(tc, w_words, w_scales, d, z, out
             nc.tensor.matmul(bank[:], lhsT=warm[:, 0:P], rhs=warm[:], start=True, stop=True)
         free_banks.append(b)
 
-        d_all = sb("d_all", [P, PASSES, 2, 2 * P], BF16)
-        d_words = d_rows[:].bitcast(F32)
-        for u in range(2):
-            b, bank = take_bank([P, 4, P], F32)
-            for a in range(4):
-                w = 2 * a + u
-                nc.tensor.transpose(bank[:, a, :], d_words[:, w:w + 1].to_broadcast([P, P]), ident[:])
-            nc.scalar.copy(out=d_all[:, :, u, :].bitcast(F32).rearrange("m c (s a) -> m c s a", a=4),
-                           in_=bank[:].rearrange("m a (c s) -> m c s a", c=PASSES))
-            free_banks.append(b)
-
         z_grouped = [[sb("z_grouped%d_%d" % (g, h), [P, HALF, PACK], BF16) for h in range(2)] for g in range(PASSES)]
-        z_codes = [[sb("z_codes%d_%d" % (g, h), [P, HALF], U32) for h in range(2)] for g in range(PASSES)]
-        z_scales = [[sb("z_scales%d_%d" % (g, h), [P, HALF], U8) for h in range(2)] for g in range(PASSES)]
+        z_codes = [sb("z_codes%d" % g, [P, R], U32) for g in range(PASSES)]
+        z_scales = [sb("z_scales%d" % g, [P, R], U8) for g in range(PASSES)]
 
         def interleave(copy, dst, src):
             copy(out=dst.rearrange("p (c i) t -> p c t i", i=4), in_=src.rearrange("p t (c i) -> p c t i", i=4))
@@ -122,36 +114,49 @@ def tile_hutchinson_squared_diagonal_s13_kernel(tc, w_words, w_scales, d, z, out
         def quantize(codes, scales, grouped):
             nc.vector.quantize_mx(out=codes.bitcast(FP8X4), scales=scales, in_=grouped.rearrange("p r t -> p (r t)"))
 
-        for h in range(2):
-            for q in range(2):
-                cols = slice(q * P, (q + 1) * P)
-                interleave(nc.vector.tensor_copy, z_grouped[0][h][:, cols, :], z0_raw[h][:, :, cols])
-            for q in range(2):
-                cols = slice(q * P, (q + 1) * P)
-                quantize(z_codes[0][h][:, cols], z_scales[0][h][:, cols], z_grouped[0][h][:, cols, :])
-        for g in range(1, PASSES):
-            interleave(nc.vector.tensor_copy, z_grouped[g][0][:], z_raw[g][:, :, 0:HALF])
-            interleave(nc.scalar.copy, z_grouped[g][1][:], z_raw[g][:, :, HALF:R])
-            for h in range(2):
-                quantize(z_codes[g][h][:], z_scales[g][h][:], z_grouped[g][h][:])
+        def quantize_rows(raw, grouped, codes, scales, pieces):
+            width = HALF // pieces
+            interleave(nc.scalar.copy, grouped[1][:], raw[:, :, HALF:R])
+            for q in range(pieces):
+                cols = slice(q * width, (q + 1) * width)
+                interleave(nc.vector.tensor_copy, grouped[0][:, cols, :], raw[:, :, cols])
+            for q in range(pieces):
+                cols = slice(q * width, (q + 1) * width)
+                quantize(codes[:, cols], scales[:, cols], grouped[0][:, cols, :])
+            quantize(codes[:, HALF:R], scales[:, HALF:R], grouped[1][:])
 
-        x_t = [[sb("x_t%d_%d" % (c, i), [P, CHUNK], BF16) for i in range(R_TILES)] for c in range(PASSES)]
+        quantize_rows(z_raw[0], z_grouped[0], z_codes[0], z_scales[0], 2)
+
+        d_all = sb("d_all", [P, 2, TURNED * 2 * P], BF16)
+        d_words = d_rows[:].bitcast(F32)
+        for u in range(2):
+            b, bank = take_bank([P, TURNED, P], F32)
+            for a in range(TURNED):
+                w = 2 * a + u
+                nc.tensor.transpose(bank[:, a, :], d_words[:, w:w + 1].to_broadcast([P, P]), ident[:])
+            nc.scalar.copy(out=d_all[:, u, :].bitcast(F32).rearrange("m (p a) -> m p a", a=TURNED),
+                           in_=bank[:].rearrange("m a p -> m p a"))
+            free_banks.append(b)
+
+        for g in range(1, PASSES):
+            quantize_rows(z_raw[g], z_grouped[g], z_codes[g], z_scales[g], 1)
+
+        x_t = [[sb("x_t%d_%d" % (c, i), [P, CHUNK], BF16) for i in range(R_TILES)] for c in range(TURNED)]
         x_grouped = [[sb("x_grouped%d_%d" % (c, h), [P, HALF, PACK], BF16) for h in range(2)] for c in range(PASSES)]
         x_codes = [sb("x_codes%d" % c, [P, R], U32) for c in range(PASSES)]
         x_scales = [sb("x_scales%d" % c, [P, R], U8) for c in range(PASSES)]
 
         def y_pass(bank, c, i, g):
-            h, q = divmod(i, 2)
-            cols = slice(q * P, (q + 1) * P)
+            cols = slice(i * P, (i + 1) * P)
             w_codes, w_scale = w_operand(g, c * CHUNK, CHUNK)
-            nc.tensor.matmul_mx(out=bank[:], lhsT=z_codes[g][h][:, cols].bitcast(FP8X4), lhsT_scale=z_scales[g][h][:, cols],
+            nc.tensor.matmul_mx(out=bank[:], lhsT=z_codes[g][:, cols].bitcast(FP8X4), lhsT_scale=z_scales[g][:, cols],
                                 rhs=w_codes, rhs_scale=w_scale, start=(g == 0), stop=(g == PASSES - 1))
 
         def y_out(b, bank, c, i):
             nc.vector.tensor_tensor(
                 out=x_t[c][i][:].rearrange("r (u p e) -> r u p e", u=2, e=2),
                 in0=bank[:].rearrange("r (p u e) -> r u p e", u=2, e=2),
-                in1=d_all[:, c].rearrange("r u (p e) -> r u p e", e=2),
+                in1=d_all[:, :, c * 2 * P:(c + 1) * 2 * P].rearrange("r u (p e) -> r u p e", e=2),
                 op=MULT)
             free_banks.append(b)
 
@@ -161,14 +166,14 @@ def tile_hutchinson_squared_diagonal_s13_kernel(tc, w_words, w_scales, d, z, out
                 y_pass(bank, c, i, g)
             y_out(b, bank, c, i)
 
-        def turn(c, copies):
+        def turn(c):
             for h in range(2):
                 b, bank = take_bank([P, 2, 2, P], F32)
                 for q in range(2):
                     words = x_t[c][2 * h + q][:].bitcast(F32)
                     for u in range(2):
                         nc.tensor.transpose(bank[:, q, u, :], words[:, u * P:(u + 1) * P], ident[:])
-                copies[h](out=x_grouped[c][h][:].bitcast(F32).rearrange("p (q r) u -> p q r u", q=2),
+                nc.scalar.copy(out=x_grouped[c][h][:].bitcast(F32).rearrange("p (q r) u -> p q r u", q=2),
                           in_=bank[:].rearrange("p q u r -> p q r u"))
                 free_banks.append(b)
 
@@ -190,20 +195,30 @@ def tile_hutchinson_squared_diagonal_s13_kernel(tc, w_words, w_scales, d, z, out
                 y_pass(sweep[c, i][1], c, i, PASSES - 1)
                 y_out(*sweep[c, i], c, i)
 
-        on_scalar = [nc.scalar.copy, nc.scalar.copy]
-        for i in range(R_TILES - 1):
+        for i in range(R_TILES):
             y_group(2, i)
-        turn(0, on_scalar)
-        turn(1, on_scalar)
-        quantize_x(0)
-        y_group(2, R_TILES - 1)
-        quantize_x(1)
-        y_group(3, 0)
-        y_group(3, 1)
-        turn(2, on_scalar)
-        quantize_x(2)
-        y_group(3, 2)
-        y_group(3, 3)
+        for c in range(TURNED):
+            turn(c)
+
+        dealt = [sb("dealt%d" % t, [P, PASSES, P], U16) for t in range(PACK)]
+        dealt_scales = [sb("dealt_scales%d" % t, [P, PASSES, P], U8) for t in range(PACK)]
+        for t in range(PACK):
+            nc.vector.tensor_copy(out=dealt[t][:],
+                                  in_=w_hi[1][:].bitcast(U16).rearrange("p g (m t) -> p t g m", t=PACK)[:, t])
+            nc.vector.tensor_copy(out=dealt_scales[t][:],
+                                  in_=ws_hi[:, :, CHUNK:2 * CHUNK].rearrange("p g (m t) -> p t g m", t=PACK)[:, t])
+        for c in range(TURNED):
+            quantize_x(c)
+        x_last = sb("x_last", [P, PACK, R], BF16)
+        for t in range(PACK):
+            b, bank = take_bank([P, R], F32)
+            for g in range(PASSES):
+                nc.tensor.matmul_mx(out=bank[:], lhsT=dealt[t][:, g, :].bitcast(FP4X4), lhsT_scale=dealt_scales[t][:, g, :],
+                                    rhs=z_codes[g][:].bitcast(FP8X4), rhs_scale=z_scales[g][:],
+                                    start=(g == 0), stop=(g == PASSES - 1))
+            nc.scalar.activation(out=x_last[:, t, :], in_=bank[:], func=COPY, scale=d_last32[:, t:t + 1])
+            free_banks.append(b)
+        quantize_rows(x_last, x_grouped[TURNED], x_codes[TURNED], x_scales[TURNED], 1)
 
         def v_pass(bank, j, g):
             w_codes, w_scale = w_operand(g, j * P, P)
@@ -223,9 +238,6 @@ def tile_hutchinson_squared_diagonal_s13_kernel(tc, w_words, w_scales, d, z, out
             early.append(take_bank([P, R], F32))
             for g in range(PASSES - 1):
                 v_pass(early[j][1], j, g)
-            if j == 0:
-                turn(3, [nc.scalar.copy, nc.vector.tensor_copy])
-                quantize_x(3)
         for j in range(4):
             v_pass(early[j][1], j, PASSES - 1)
             v_out(*early[j], j)

@@ -23,7 +23,6 @@ R_TILES = R // P
 HALF = R // 2
 N_TILES = N // P
 BANKS = 8
-WARMUPS = 4
 TURNED = PASSES - 1
 U16 = mybir.dt.uint16
 COPY = mybir.ActivationFunctionType.Copy
@@ -40,7 +39,7 @@ def tile_hutchinson_squared_diagonal_s13_kernel(tc, w_words, w_scales, d, z, out
         def sb(name, shape, dtype):
             return keep.tile(shape, dtype, name=name, align_bytes=64)
 
-        free_banks = [BANKS - 3, BANKS - 2, BANKS - 1] + list(range(BANKS - 3))
+        free_banks = [BANKS - 2, BANKS - 1] + list(range(BANKS - 2))
 
         def take_bank(shape, dtype):
             b = free_banks[0]
@@ -51,8 +50,7 @@ def tile_hutchinson_squared_diagonal_s13_kernel(tc, w_words, w_scales, d, z, out
         d_last = sb("d_last", [P, PACK], BF16)
         d_last32 = sb("d_last32", [P, PACK], F32)
         ws_lo = [sb("ws_lo%d" % h, [P, 2, N // 2], U8) for h in range(2)]
-        ws_hi = sb("ws_hi", [P, PASSES, N // 2], U8)
-        warm = sb("warm", [P, CHUNK], BF16)
+        ws_hi = [sb("ws_hi%d" % c, [P, PASSES, CHUNK], U8) for c in range(2)]
         sums = sb("sums", [P, 32], F32)
         ident = sb("ident", [P, P], F32)
         z_raw = [sb("z_raw%d" % g, [P, PACK, R], BF16) for g in range(PASSES)]
@@ -60,10 +58,8 @@ def tile_hutchinson_squared_diagonal_s13_kernel(tc, w_words, w_scales, d, z, out
         w_hi = [sb("w_hi%d" % c, [P, PASSES, 2 * CHUNK], U8) for c in range(2)]
         z_rows = [sb("z_rows%d" % c, [P, PACK, R], BF16) for c in range(PASSES)]
 
-        nc.gpsimd.memset(warm[:].bitcast(I32), 0)
-        nc.vector.memset(ws_lo[0][:].bitcast(I32), 0)
-        nc.vector.memset(ws_lo[1][:].bitcast(I32), 0)
-        nc.vector.memset(ws_hi[:].bitcast(I32), 0)
+        for plane in ws_lo + ws_hi:
+            nc.vector.memset(plane[:].bitcast(I32), 0)
         nc.vector.memset(sums[:], 0.0)
         make_identity(nc, ident[:])
 
@@ -83,8 +79,8 @@ def tile_hutchinson_squared_diagonal_s13_kernel(tc, w_words, w_scales, d, z, out
             if g % 2 == 0:
                 load_scales(ws_lo[g // 2], slice(g, g + 2), slice(0, N // 2))
             nc.sync.dma_start(out=w_lo[g][:].bitcast(I32), in_=w_words[g][:, 0:N].bitcast(I32))
-        load_scales(ws_hi, slice(0, PASSES), slice(N // 2, N))
         for c in range(2):
+            load_scales(ws_hi[c], slice(0, PASSES), slice(N // 2 + c * CHUNK, N // 2 + (c + 1) * CHUNK))
             cols = slice(N + c * 2 * CHUNK, N + (c + 1) * 2 * CHUNK)
             nc.sync.dma_start(out=w_hi[c][:].bitcast(I32),
                               in_=w_words.rearrange("g p b -> p g b")[:, :, cols].bitcast(I32))
@@ -97,12 +93,7 @@ def tile_hutchinson_squared_diagonal_s13_kernel(tc, w_words, w_scales, d, z, out
             if h == 0:
                 return w_lo[g][:, 2 * n1:2 * (n1 + width)].bitcast(FP4X4), ws_lo[g // 2][:, g % 2, n1:n1 + width]
             c, n2 = divmod(n1, CHUNK)
-            return w_hi[c][:, g, 2 * n2:2 * (n2 + width)].bitcast(FP4X4), ws_hi[:, g, n1:n1 + width]
-
-        b, bank = take_bank([P, CHUNK], F32)
-        for w in range(WARMUPS):
-            nc.tensor.matmul(bank[:], lhsT=warm[:, 0:P], rhs=warm[:], start=True, stop=True)
-        free_banks.append(b)
+            return w_hi[c][:, g, 2 * n2:2 * (n2 + width)].bitcast(FP4X4), ws_hi[c][:, g, n2:n2 + width]
 
         z_grouped = [[sb("z_grouped%d_%d" % (g, h), [P, HALF, PACK], BF16) for h in range(2)] for g in range(PASSES)]
         z_codes = [sb("z_codes%d" % g, [P, R], U32) for g in range(PASSES)]
@@ -114,18 +105,17 @@ def tile_hutchinson_squared_diagonal_s13_kernel(tc, w_words, w_scales, d, z, out
         def quantize(codes, scales, grouped):
             nc.vector.quantize_mx(out=codes.bitcast(FP8X4), scales=scales, in_=grouped.rearrange("p r t -> p (r t)"))
 
-        def quantize_rows(raw, grouped, codes, scales, pieces):
-            width = HALF // pieces
+        def quantize_rows(raw, grouped, codes, scales):
             interleave(nc.scalar.copy, grouped[1][:], raw[:, :, HALF:R])
-            for q in range(pieces):
-                cols = slice(q * width, (q + 1) * width)
+            for q in range(2):
+                cols = slice(q * P, (q + 1) * P)
                 interleave(nc.vector.tensor_copy, grouped[0][:, cols, :], raw[:, :, cols])
-            for q in range(pieces):
-                cols = slice(q * width, (q + 1) * width)
+            for q in range(2):
+                cols = slice(q * P, (q + 1) * P)
                 quantize(codes[:, cols], scales[:, cols], grouped[0][:, cols, :])
             quantize(codes[:, HALF:R], scales[:, HALF:R], grouped[1][:])
 
-        quantize_rows(z_raw[0], z_grouped[0], z_codes[0], z_scales[0], 2)
+        quantize_rows(z_raw[0], z_grouped[0], z_codes[0], z_scales[0])
 
         d_all = sb("d_all", [P, 2, TURNED * 2 * P], BF16)
         d_words = d_rows[:].bitcast(F32)
@@ -139,7 +129,7 @@ def tile_hutchinson_squared_diagonal_s13_kernel(tc, w_words, w_scales, d, z, out
             free_banks.append(b)
 
         for g in range(1, PASSES):
-            quantize_rows(z_raw[g], z_grouped[g], z_codes[g], z_scales[g], 1)
+            quantize_rows(z_raw[g], z_grouped[g], z_codes[g], z_scales[g])
 
         x_t = [[sb("x_t%d_%d" % (c, i), [P, CHUNK], BF16) for i in range(R_TILES)] for c in range(TURNED)]
         x_grouped = [[sb("x_grouped%d_%d" % (c, h), [P, HALF, PACK], BF16) for h in range(2)] for c in range(PASSES)]
@@ -206,7 +196,7 @@ def tile_hutchinson_squared_diagonal_s13_kernel(tc, w_words, w_scales, d, z, out
             nc.vector.tensor_copy(out=dealt[t][:],
                                   in_=w_hi[1][:].bitcast(U16).rearrange("p g (m t) -> p t g m", t=PACK)[:, t])
             nc.vector.tensor_copy(out=dealt_scales[t][:],
-                                  in_=ws_hi[:, :, CHUNK:2 * CHUNK].rearrange("p g (m t) -> p t g m", t=PACK)[:, t])
+                                  in_=ws_hi[1][:].rearrange("p g (m t) -> p t g m", t=PACK)[:, t])
         for c in range(TURNED):
             quantize_x(c)
         x_last = sb("x_last", [P, PACK, R], BF16)
@@ -218,7 +208,7 @@ def tile_hutchinson_squared_diagonal_s13_kernel(tc, w_words, w_scales, d, z, out
                                     start=(g == 0), stop=(g == PASSES - 1))
             nc.scalar.activation(out=x_last[:, t, :], in_=bank[:], func=COPY, scale=d_last32[:, t:t + 1])
             free_banks.append(b)
-        quantize_rows(x_last, x_grouped[TURNED], x_codes[TURNED], x_scales[TURNED], 1)
+        quantize_rows(x_last, x_grouped[TURNED], x_codes[TURNED], x_scales[TURNED])
 
         def v_pass(bank, j, g):
             w_codes, w_scale = w_operand(g, j * P, P)
@@ -233,14 +223,12 @@ def tile_hutchinson_squared_diagonal_s13_kernel(tc, w_words, w_scales, d, z, out
             nc.sync.dma_start(out=out_0[j * P:(j + 1) * P, :], in_=c_tile[:])
             free_banks.append(b)
 
-        early = []
-        for j in range(4):
-            early.append(take_bank([P, R], F32))
-            for g in range(PASSES - 1):
+        early = [take_bank([P, R], F32) for j in range(4)]
+        for g in range(PASSES):
+            for j in range(4):
                 v_pass(early[j][1], j, g)
-        for j in range(4):
-            v_pass(early[j][1], j, PASSES - 1)
-            v_out(*early[j], j)
+                if g == PASSES - 1:
+                    v_out(*early[j], j)
         for j in range(4, N_TILES):
             b, bank = take_bank([P, R], F32)
             for g in range(PASSES):

from contextlib import ExitStack

import concourse.mybir as mybir
from concourse.masks import make_identity

N, R = 2048, 512
FLOPS = 2 * 2 * N * N * R

F32 = mybir.dt.float32
BF16 = mybir.dt.bfloat16
I32 = mybir.dt.int32
U32 = mybir.dt.uint32
U8 = mybir.dt.uint8
FP8X4 = mybir.dt.float8_e4m3fn_x4
FP4X4 = mybir.dt.float4_e2m1fn_x4
MULT = mybir.AluOpType.mult

P = 128
PACK = 4
CHUNK = P * PACK
PASSES = N // CHUNK
R_TILES = R // P
HALF = R // 2
N_TILES = N // P
BANKS = 8
TURNED = PASSES - 1
U16 = mybir.dt.uint16
COPY = mybir.ActivationFunctionType.Copy


def tile_hutchinson_squared_diagonal_s13_kernel(tc, w_words, w_scales, d, z, out_0, out_1):
    nc = tc.nc
    with ExitStack() as ctx:
        keep = ctx.enter_context(tc.tile_pool(name="keep", bufs=1))
        stage = ctx.enter_context(tc.tile_pool(name="stage", bufs=6))
        psum = ctx.enter_context(tc.psum_pool(name="psum", bufs=1))
        ctx.enter_context(tc.manual_schedule())

        def sb(name, shape, dtype):
            return keep.tile(shape, dtype, name=name, align_bytes=64)

        free_banks = [BANKS - 2, BANKS - 1] + list(range(BANKS - 2))

        def take_bank(shape, dtype):
            b = free_banks[0]
            free_banks.remove(b)
            return b, psum.tile(shape, dtype, name="bank%d" % b, tag="bank%d" % b)

        d_rows = sb("d_rows", [P, PACK * TURNED], BF16)
        d_last = sb("d_last", [P, PACK], BF16)
        d_last32 = sb("d_last32", [P, PACK], F32)
        ws_lo = [sb("ws_lo%d" % h, [P, 2, N // 2], U8) for h in range(2)]
        ws_hi = [sb("ws_hi%d" % c, [P, PASSES, CHUNK], U8) for c in range(2)]
        sums = sb("sums", [P, 32], F32)
        ident = sb("ident", [P, P], F32)
        z_raw = [sb("z_raw%d" % g, [P, PACK, R], BF16) for g in range(PASSES)]
        w_lo = [sb("w_lo%d" % g, [P, N], U8) for g in range(PASSES)]
        w_hi = [sb("w_hi%d" % c, [P, PASSES, 2 * CHUNK], U8) for c in range(2)]
        z_rows = [sb("z_rows%d" % c, [P, PACK, R], BF16) for c in range(PASSES)]

        for plane in ws_lo + ws_hi:
            nc.vector.memset(plane[:].bitcast(I32), 0)
        nc.vector.memset(sums[:], 0.0)
        make_identity(nc, ident[:])

        def z_pass(g):
            return z[g * CHUNK:(g + 1) * CHUNK, :].rearrange("(p t) r -> p t r", t=PACK)

        def load_scales(plane, passes, cols):
            rows = w_scales.rearrange("g (q s) n -> s q g n", s=4)
            for s in range(4):
                nc.sync.dma_start(out=plane[s:P:32].bitcast(I32), in_=rows[s][:, passes, cols].bitcast(I32))

        nc.scalar.dma_start(out=d_rows[:], in_=d[0:TURNED * CHUNK].rearrange("(p j) -> p j", p=P))
        nc.scalar.dma_start(out=d_last[:], in_=d[TURNED * CHUNK:N].rearrange("(p t) -> p t", p=P))
        nc.scalar.activation(out=d_last32[:], in_=d_last[:], func=COPY)
        for g in range(PASSES):
            nc.sync.dma_start(out=z_raw[g][:], in_=z_pass(g))
            if g % 2 == 0:
                load_scales(ws_lo[g // 2], slice(g, g + 2), slice(0, N // 2))
            nc.sync.dma_start(out=w_lo[g][:].bitcast(I32), in_=w_words[g][:, 0:N].bitcast(I32))
        for c in range(2):
            load_scales(ws_hi[c], slice(0, PASSES), slice(N // 2 + c * CHUNK, N // 2 + (c + 1) * CHUNK))
            cols = slice(N + c * 2 * CHUNK, N + (c + 1) * 2 * CHUNK)
            nc.sync.dma_start(out=w_hi[c][:].bitcast(I32),
                              in_=w_words.rearrange("g p b -> p g b")[:, :, cols].bitcast(I32))
        for c in range(PASSES):
            nc.sync.dma_start(out=z_rows[c][:],
                              in_=z[c * CHUNK:(c + 1) * CHUNK, :].rearrange("(j p) r -> p j r", p=P))

        def w_operand(g, n0, width):
            h, n1 = divmod(n0, N // 2)
            if h == 0:
                return w_lo[g][:, 2 * n1:2 * (n1 + width)].bitcast(FP4X4), ws_lo[g // 2][:, g % 2, n1:n1 + width]
            c, n2 = divmod(n1, CHUNK)
            return w_hi[c][:, g, 2 * n2:2 * (n2 + width)].bitcast(FP4X4), ws_hi[c][:, g, n2:n2 + width]

        z_grouped = [[sb("z_grouped%d_%d" % (g, h), [P, HALF, PACK], BF16) for h in range(2)] for g in range(PASSES)]
        z_codes = [sb("z_codes%d" % g, [P, R], U32) for g in range(PASSES)]
        z_scales = [sb("z_scales%d" % g, [P, R], U8) for g in range(PASSES)]

        def interleave(copy, dst, src):
            copy(out=dst.rearrange("p (c i) t -> p c t i", i=4), in_=src.rearrange("p t (c i) -> p c t i", i=4))

        def quantize(codes, scales, grouped):
            nc.vector.quantize_mx(out=codes.bitcast(FP8X4), scales=scales, in_=grouped.rearrange("p r t -> p (r t)"))

        def quantize_rows(raw, grouped, codes, scales):
            interleave(nc.scalar.copy, grouped[1][:], raw[:, :, HALF:R])
            for q in range(2):
                cols = slice(q * P, (q + 1) * P)
                interleave(nc.vector.tensor_copy, grouped[0][:, cols, :], raw[:, :, cols])
            for q in range(2):
                cols = slice(q * P, (q + 1) * P)
                quantize(codes[:, cols], scales[:, cols], grouped[0][:, cols, :])
            quantize(codes[:, HALF:R], scales[:, HALF:R], grouped[1][:])

        quantize_rows(z_raw[0], z_grouped[0], z_codes[0], z_scales[0])

        d_all = sb("d_all", [P, 2, TURNED * 2 * P], BF16)
        d_words = d_rows[:].bitcast(F32)
        for u in range(2):
            b, bank = take_bank([P, TURNED, P], F32)
            for a in range(TURNED):
                w = 2 * a + u
                nc.tensor.transpose(bank[:, a, :], d_words[:, w:w + 1].to_broadcast([P, P]), ident[:])
            nc.scalar.copy(out=d_all[:, u, :].bitcast(F32).rearrange("m (p a) -> m p a", a=TURNED),
                           in_=bank[:].rearrange("m a p -> m p a"))
            free_banks.append(b)

        for g in range(1, PASSES):
            quantize_rows(z_raw[g], z_grouped[g], z_codes[g], z_scales[g])

        x_t = [[sb("x_t%d_%d" % (c, i), [P, CHUNK], BF16) for i in range(R_TILES)] for c in range(TURNED)]
        x_grouped = [[sb("x_grouped%d_%d" % (c, h), [P, HALF, PACK], BF16) for h in range(2)] for c in range(PASSES)]
        x_codes = [sb("x_codes%d" % c, [P, R], U32) for c in range(PASSES)]
        x_scales = [sb("x_scales%d" % c, [P, R], U8) for c in range(PASSES)]

        def y_pass(bank, c, i, g):
            cols = slice(i * P, (i + 1) * P)
            w_codes, w_scale = w_operand(g, c * CHUNK, CHUNK)
            nc.tensor.matmul_mx(out=bank[:], lhsT=z_codes[g][:, cols].bitcast(FP8X4), lhsT_scale=z_scales[g][:, cols],
                                rhs=w_codes, rhs_scale=w_scale, start=(g == 0), stop=(g == PASSES - 1))

        def y_out(b, bank, c, i):
            nc.vector.tensor_tensor(
                out=x_t[c][i][:].rearrange("r (u p e) -> r u p e", u=2, e=2),
                in0=bank[:].rearrange("r (p u e) -> r u p e", u=2, e=2),
                in1=d_all[:, :, c * 2 * P:(c + 1) * 2 * P].rearrange("r u (p e) -> r u p e", e=2),
                op=MULT)
            free_banks.append(b)

        def y_group(c, i):
            b, bank = take_bank([P, CHUNK], F32)
            for g in range(PASSES):
                y_pass(bank, c, i, g)
            y_out(b, bank, c, i)

        def turn(c):
            for h in range(2):
                b, bank = take_bank([P, 2, 2, P], F32)
                for q in range(2):
                    words = x_t[c][2 * h + q][:].bitcast(F32)
                    for u in range(2):
                        nc.tensor.transpose(bank[:, q, u, :], words[:, u * P:(u + 1) * P], ident[:])
                nc.scalar.copy(out=x_grouped[c][h][:].bitcast(F32).rearrange("p (q r) u -> p q r u", q=2),
                          in_=bank[:].rearrange("p q u r -> p q r u"))
                free_banks.append(b)

        def quantize_x(c):
            for h in range(2):
                cols = slice(h * HALF, (h + 1) * HALF)
                quantize(x_codes[c][:, cols], x_scales[c][:, cols], x_grouped[c][h][:])

        sweep = {}
        for i in range(R_TILES):
            for c in range(2):
                sweep[c, i] = take_bank([P, CHUNK], F32)
        for g in range(PASSES - 1):
            for i in range(R_TILES):
                for c in range(2):
                    y_pass(sweep[c, i][1], c, i, g)
        for c in range(2):
            for i in range(R_TILES):
                y_pass(sweep[c, i][1], c, i, PASSES - 1)
                y_out(*sweep[c, i], c, i)

        for i in range(R_TILES):
            y_group(2, i)
        for c in range(TURNED):
            turn(c)

        dealt = [sb("dealt%d" % t, [P, PASSES, P], U16) for t in range(PACK)]
        dealt_scales = [sb("dealt_scales%d" % t, [P, PASSES, P], U8) for t in range(PACK)]
        for t in range(PACK):
            nc.vector.tensor_copy(out=dealt[t][:],
                                  in_=w_hi[1][:].bitcast(U16).rearrange("p g (m t) -> p t g m", t=PACK)[:, t])
            nc.vector.tensor_copy(out=dealt_scales[t][:],
                                  in_=ws_hi[1][:].rearrange("p g (m t) -> p t g m", t=PACK)[:, t])
        for c in range(TURNED):
            quantize_x(c)
        x_last = sb("x_last", [P, PACK, R], BF16)
        for t in range(PACK):
            b, bank = take_bank([P, R], F32)
            for g in range(PASSES):
                nc.tensor.matmul_mx(out=bank[:], lhsT=dealt[t][:, g, :].bitcast(FP4X4), lhsT_scale=dealt_scales[t][:, g, :],
                                    rhs=z_codes[g][:].bitcast(FP8X4), rhs_scale=z_scales[g][:],
                                    start=(g == 0), stop=(g == PASSES - 1))
            nc.scalar.activation(out=x_last[:, t, :], in_=bank[:], func=COPY, scale=d_last32[:, t:t + 1])
            free_banks.append(b)
        quantize_rows(x_last, x_grouped[TURNED], x_codes[TURNED], x_scales[TURNED])

        def v_pass(bank, j, g):
            w_codes, w_scale = w_operand(g, j * P, P)
            nc.tensor.matmul_mx(out=bank[:], lhsT=w_codes, lhsT_scale=w_scale,
                                rhs=x_codes[g][:].bitcast(FP8X4), rhs_scale=x_scales[g][:],
                                start=(g == 0), stop=(g == PASSES - 1))

        def v_out(b, bank, j):
            c_tile = stage.tile([P, R], F32, name="c_tile")
            nc.vector.scalar_tensor_tensor(out=c_tile[:], in0=bank[:], scalar=1.0, in1=z_rows[j // PACK][:, j % PACK, :],
                                           op0=MULT, op1=MULT, accum_out=sums[:, j:j + 1])
            nc.sync.dma_start(out=out_0[j * P:(j + 1) * P, :], in_=c_tile[:])
            free_banks.append(b)

        early = [take_bank([P, R], F32) for j in range(4)]
        for g in range(PASSES):
            for j in range(4):
                v_pass(early[j][1], j, g)
                if g == PASSES - 1:
                    v_out(*early[j], j)
        for j in range(4, N_TILES):
            b, bank = take_bank([P, R], F32)
            for g in range(PASSES):
                v_pass(bank, j, g)
            v_out(b, bank, j)

        means = sb("means", [P, 32], F32)
        means_t = sb("means_t", [P, 32], F32)
        nc.vector.tensor_scalar(out=means[:], in0=sums[:], scalar1=1.0 / R, scalar2=None, op0=MULT)
        nc.vector.transpose(means_t[:], means[:])
        d_out = out_1.rearrange("(j q i) -> q j i", q=4, i=32)
        for q in range(4):
            queue = nc.scalar if q % 2 == 0 else nc.sync
            queue.dma_start(out=d_out[q], in_=means_t[32 * q:32 * q + N_TILES, :])
